import numpy as np
import ml_dtypes


def mxq(x, axis, fmt="e4m3"):
    dtype, down = {"e4m3": (ml_dtypes.float8_e4m3fn, 7), "e5m2": (ml_dtypes.float8_e5m2, 14)}[fmt]
    v = np.moveaxis(np.asarray(x, np.float32).astype(ml_dtypes.bfloat16).astype(np.float64), axis, -1)
    blocks = v.reshape(v.shape[:-1] + (-1, 32))
    amax = np.abs(blocks).max(-1, keepdims=True)
    byte = np.maximum(np.where(amax > 0, np.frexp(amax)[1] - 1 + 127, 0) - down, 1)
    scale = np.exp2(byte - 127.0)
    codes = (blocks / scale).astype(np.float32).astype(dtype).astype(np.float64)
    return np.moveaxis((codes * scale).reshape(v.shape), -1, axis)


WIDE = False


def mx_kscale(k):
    if not WIDE:
        return np.ones(k)
    levels = np.array([10, -10, 5, -5, 0])
    if k % 512:
        return np.exp2(np.random.permutation(np.resize(levels, k // 32))).repeat(32)
    a = np.empty((k // 512, 16))
    for p in range(k // 512):
        a[p, :8] = np.random.permutation(np.resize(levels, 8))
        for g in range(8):
            far = levels[np.abs(levels - a[p, g]) >= 10]
            a[p, g + 8] = far[np.random.randint(len(far))]
    return np.exp2(a.ravel()).repeat(32)


def f64(x):
    return np.asarray(x).astype(np.float64)


def striped(idx):
    return np.tile(idx.reshape(-1, 16).T, (8, 1)).astype(np.uint16)


def unstriped(offs):
    return offs[:16].T.reshape(-1).astype(np.int64)


def striped8(idx):
    return np.concatenate([x.reshape(-1, 16).T for x in idx]).astype(np.uint16)


def runs(offs, k):
    lists = np.stack([offs[16 * r : 16 * r + 16].T.reshape(-1) for r in range(8)]).astype(np.int64)
    return lists[np.arange(k) % 512 // 64]


def pack_weight(w):
    k, n = w.shape
    w = f64(np.asarray(w, np.float32).astype(ml_dtypes.bfloat16)).reshape(k // 32, 32, n)
    amax = np.abs(w).max(1)
    byte = np.clip(np.where(amax > 0, np.frexp(amax)[1] - 1 + 127 - 7, 1), 1, 254)
    scaled = (w * np.exp2(127.0 - byte)[:, None, :]).reshape(k, n).astype(np.float32)
    words = np.ascontiguousarray(scaled.reshape(k // 512, 128, 4, n).transpose(0, 1, 3, 2)).astype(ml_dtypes.float8_e4m3fn).view(np.uint8)
    return words, np.ascontiguousarray(byte.astype(np.uint8).reshape(k // 512, 16, n))


def unpack_weight(words, scales):
    g, p, n, _ = words.shape
    vals = np.ascontiguousarray(words).view(ml_dtypes.float8_e4m3fn).astype(np.float64) * np.repeat(np.exp2(scales.astype(np.float64) - 127.0), 8, axis=1)[..., None]
    return vals.transpose(0, 1, 3, 2).reshape(g * 512, n)


def sigmoid(v):
    return 1.0 / (1.0 + np.exp(-np.maximum(v, -700.0)))


K, T, S, V, H, W = 512, 2048, 512, 512, 512, 256


def setup_inputs():
    n = np.random.standard_normal
    s = mx_kscale(K)[:, None]
    u = mx_kscale(S)
    packed_xT = pack_weight(n((K, T)) * s)
    perm = np.stack([np.random.permutation(S) for _ in range(8)])
    return {
        "x_words": packed_xT[0],
        "x_scales": packed_xT[1],
        "w1": (n((K, H)) / np.sqrt(K) / s).astype(np.float32),
        "w2": (n((K, H)) / np.sqrt(K) / s).astype(np.float32),
        "ga": (np.random.uniform(0.5, 1.5, (H, 1)) * u[:, None]).astype(np.float32),
        "gb": (np.random.uniform(0.5, 1.5, (H, 1)) / u[:, None]).astype(np.float32),
        "offs": striped(np.random.permutation(T)[:S]),
        "two": striped(np.random.permutation(T)[:V]),
        "n1": striped8(perm[:, :W]),
        "n2": striped8(perm[:, W:]),
        "n3": striped8(np.stack([np.random.permutation(V) for _ in range(8)])),
        "n4": striped8(np.stack([np.random.permutation(V) for _ in range(8)])),
        "n5": striped8(np.stack([np.random.permutation(V) for _ in range(8)])),
        "n6": striped8(np.stack([np.random.permutation(V) for _ in range(8)])),
    }


def reference(x_words, x_scales, w1, w2, ga, gb, offs, two, n1, n2, n3, n4, n5, n6):
    xq = unpack_weight(x_words, x_scales)[:, unstriped(offs)]
    a = mxq(f64(w1), 0, "e4m3").T @ xq
    pa = a[np.arange(H)[:, None], runs(n1, H)]
    pb = a[np.arange(H)[:, None], runs(n2, H)]
    rb = np.maximum(pa, pb)
    ra = pa / (np.abs(pb) + 0.5)
    ds = np.zeros((H, S))
    ds[np.arange(H)[:, None], runs(n1, H)] = ra
    dt = ds.copy()
    dt[np.arange(H)[:, None], runs(n2, H)] = rb
    z = f64(ga) * dt
    x_two = unpack_weight(x_words, x_scales)[:, unstriped(two)]
    b = mxq(f64(w2), 0, "e4m3").T @ x_two
    z2 = f64(gb) * (np.maximum(b[np.arange(H)[:, None], runs(n3, H)], b[np.arange(H)[:, None], runs(n4, H)]) - (0.75 * b))
    s = 0.0625 * ((mxq(z, 0, "e4m3").T @ mxq(z2, 0, "e4m3")))
    return s * (sigmoid(s[np.arange(S)[:, None], runs(n5, S)] - (s[np.arange(S)[:, None], runs(n6, S)])))

@@ -1,0 +1,214 @@
+from contextlib import ExitStack
+
+import concourse.mybir as mybir
+
+F32 = mybir.dt.float32
+BF16 = mybir.dt.bfloat16
+U32 = mybir.dt.uint32
+I32 = mybir.dt.int32
+U16 = mybir.dt.uint16
+U8 = mybir.dt.uint8
+FP8X4 = mybir.dt.float8_e4m3fn_x4
+ALU = mybir.AluOpType
+ACT = mybir.ActivationFunctionType
+
+P = 128
+PACK = 4
+K, T, S, V, H, W = 512, 2048, 512, 512, 512, 256
+LIST_COL = 16
+FLOPS = 3 * 2 * 512 * 512 * 512
+
+QUERY_CHUNKS = ((0, 256), (256, 384), (384, 512))
+GATE_PIECES = ((0, 256), (256, 512))
+LAST_GATE_PIECES = ((0, 256), (256, 384), (384, 512))
+
+
+def tile_picked_kqratioovercmp_none_p_kernel(
+    tc, x_words, x_scales, w1, w2, ga, gb, offs, two, n1, n2, n3, n4, n5, n6, out
+):
+    nc = tc.nc
+    with ExitStack() as ctx:
+        lists = ctx.enter_context(tc.tile_pool(name="lists", bufs=1))
+        keep = ctx.enter_context(tc.tile_pool(name="keep", bufs=1))
+        psum = ctx.enter_context(tc.psum_pool(name="psum", bufs=1))
+
+        def load_list(src, name):
+            tile = lists.tile(list(src.shape), U16, name=name)
+            nc.sync.dma_start(tile[:], src)
+            return tile
+
+        def entries(tile, lo, hi):
+            return tile[:, lo // LIST_COL : hi // LIST_COL]
+
+        def load_weight(w, name):
+            halves = []
+            for h in range(2):
+                half = keep.tile([P, PACK, H // 2], F32, name="%s_raw%d" % (name, h))
+                nc.sync.dma_start(half[:], w.rearrange("(p j) c -> p j c", j=PACK)[:, :, h * (H // 2) : (h + 1) * (H // 2)])
+                halves.append(half)
+            return halves
+
+        def quantise(src, name):
+            width = src.shape[1] // PACK
+            codes = keep.tile([P, width], U32, name=name + "_codes", align_bytes=64)
+            scales = keep.tile([P, width], U8, name=name + "_scales", align_bytes=64)
+            nc.vector.quantize_mx(out=codes[:].bitcast(FP8X4), scales=scales[:], in_=src)
+            return codes, scales
+
+        def quantise_weight(halves, name):
+            grouped = keep.tile([P, PACK * H], BF16, name=name + "_bf16", tag="grouped", align_bytes=64)
+            dealt = grouped[:].rearrange("p (t m j) -> p m j t", t=PACK, j=PACK)
+            for h, half in enumerate(halves):
+                nc.scalar.copy(dealt[:, h * (P // 2) : (h + 1) * (P // 2)], half[:].rearrange("p j (m t) -> p m j t", t=PACK))
+            return quantise(grouped[:], name)
+
+        def product(bank, lhs, t, rhs):
+            cols = slice(t * P, (t + 1) * P)
+            nc.tensor.matmul_mx(
+                out=bank, lhsT=lhs[0][:, cols].bitcast(FP8X4), lhsT_scale=lhs[1][:, cols],
+                rhs=rhs[0][:].bitcast(FP8X4), rhs_scale=rhs[1][:], start=True, stop=True,
+            )
+
+        byte_table = keep.tile([P, T], U8, name="byte_table")
+        nc.vector.memset(byte_table[:].bitcast(I32), 0)
+        offs_t = load_list(offs, "offs")
+        two_t = load_list(two, "two")
+        for q in range(4):
+            nc.scalar.dma_start(byte_table[32 * q : 32 * q + 4, :].bitcast(I32), x_scales[0, 4 * q : 4 * q + 4, :].bitcast(I32))
+        w1_raw = load_weight(w1, "w1")
+        word_table = keep.tile([P, T], I32, name="word_table")
+        nc.sync.dma_start(word_table[:], x_words[0].rearrange("p c r -> p (c r)").bitcast(I32))
+        n1_t = load_list(n1, "n1")
+        n2_t = load_list(n2, "n2")
+        ga_t = keep.tile([P, PACK], F32, name="ga_t")
+        gb_t = keep.tile([P, PACK], F32, name="gb_t")
+        nc.sync.dma_start(ga_t[:], ga.rearrange("(p t) o -> p (t o)", t=PACK))
+        nc.sync.dma_start(gb_t[:], gb.rearrange("(p t) o -> p (t o)", t=PACK))
+        w2_raw = load_weight(w2, "w2")
+        n3_t = load_list(n3, "n3")
+        n4_t = load_list(n4, "n4")
+        n5_t = load_list(n5, "n5")
+        n6_t = load_list(n6, "n6")
+
+        half_col = keep.tile([P, 1], F32, name="half_col")
+        nc.vector.memset(half_col[:], 0.5)
+
+        def pick(table, dtype, offsets, name):
+            picked = keep.tile([P, S], dtype, name=name, align_bytes=64)
+            nc.vector.tensor_copy(picked[:], table.indirect(offsets[:]))
+            return picked
+
+        a_bytes = pick(byte_table[:], U8, offs_t, "a_bytes")
+        b_bytes = pick(byte_table[:], U8, two_t, "b_bytes")
+        w1_q = quantise_weight(w1_raw, "w1")
+        a_words = pick(word_table[:].bitcast(U32), U32, offs_t, "a_words")
+        b_words = pick(word_table[:].bitcast(U32), U32, two_t, "b_words")
+
+        a_rows = []
+        for t in range(PACK):
+            bank = psum.tile([P, S], F32, name="a_bank%d" % t, tag="bank%d" % t)
+            product(bank[:], w1_q, t, (a_words, a_bytes))
+            rows = keep.tile([P, S], F32, name="a_rows%d" % t)
+            nc.scalar.copy(rows[:], bank[:])
+            a_rows.append(rows)
+
+        sign_b = keep.tile([P, PACK], F32, name="sign_b")
+        nc.vector.tensor_scalar(sign_b[:], gb_t[:], 0.0, 2.0, ALU.is_ge, ALU.mult)
+        z_factor = keep.tile([P, PACK], F32, name="z_factor")
+        nc.vector.scalar_tensor_tensor(z_factor[:], sign_b[:], -1.0, ga_t[:], ALU.add, ALU.mult)
+        b_factor = keep.tile([P, PACK], F32, name="b_factor")
+        nc.vector.scalar_tensor_tensor(b_factor[:], sign_b[:], -1.0, gb_t[:], ALU.add, ALU.mult)
+        own_factor = keep.tile([P, PACK], F32, name="own_factor")
+        nc.vector.tensor_scalar(own_factor[:], b_factor[:], -0.75, None, ALU.mult)
+
+        pa = keep.tile([P, PACK, W], F32, name="pa")
+        pb = keep.tile([P, PACK, W], F32, name="pb")
+        rb = keep.tile([P, PACK, W], F32, name="rb")
+        size_b = keep.tile([P, PACK, W], F32, name="size_b")
+        root = keep.tile([P, PACK, W], F32, name="root")
+        inverse = keep.tile([P, PACK, W], F32, name="inverse")
+        dt_rows = [keep.tile([P, S], F32, name="dt_rows%d" % t) for t in range(PACK)]
+
+        def fetch_pairs(t):
+            nc.vector.tensor_copy(pb[:, t, :], a_rows[t][:].indirect(n2_t[:]))
+            nc.vector.tensor_copy(pa[:, t, :], a_rows[t][:].indirect(n1_t[:]))
+            nc.scalar.activation(size_b[:, t, :], pb[:, t, :], ACT.Abs)
+            nc.scalar.activation(root[:, t, :], size_b[:, t, :], ACT.Abs_reciprocal_sqrt, bias=half_col[:])
+            nc.scalar.activation(inverse[:, t, :], root[:, t, :], ACT.Square)
+
+        def put_larger(t):
+            nc.vector.tensor_tensor(rb[:, t, :], pa[:, t, :], pb[:, t, :], ALU.max)
+
+        def scatter_b(t):
+            nc.vector.tensor_copy(dt_rows[t][:].indirect(n2_t[:]), rb[:, t, :])
+
+        def scatter_a(t):
+            nc.vector.tensor_tensor(dt_rows[t][:].indirect(n1_t[:]), pa[:, t, :], inverse[:, t, :], ALU.mult)
+
+        fetch_pairs(0)
+        for t in range(PACK):
+            if t + 1 < PACK:
+                fetch_pairs(t + 1)
+            put_larger(t)
+            if t > 0:
+                scatter_a(t - 1)
+            scatter_b(t)
+
+        w2_q = quantise_weight(w2_raw, "w2")
+        scatter_a(PACK - 1)
+        b_rows, own_rows = [], []
+        for t in range(PACK):
+            bank = psum.tile([P, V], F32, name="b_bank%d" % t, tag="bank%d" % (PACK + t))
+            product(bank[:], w2_q, t, (b_words, b_bytes))
+            rows = keep.tile([P, V], F32, name="b_rows%d" % t)
+            nc.scalar.activation(rows[:], bank[:], ACT.Copy, scale=b_factor[:, t : t + 1])
+            own = keep.tile([P, V], F32, name="own_rows%d" % t)
+            nc.scalar.activation(own[:], bank[:], ACT.Copy, scale=own_factor[:, t : t + 1])
+            b_rows.append(rows)
+            own_rows.append(own)
+
+        z_grouped = keep.tile([P, PACK * S], BF16, name="z_bf16", tag="grouped", align_bytes=64)
+        z_dealt = z_grouped[:].rearrange("p (u m t) -> p t m u", u=PACK, t=PACK)
+        for t in range(PACK):
+            nc.scalar.activation(
+                z_dealt[:, t], dt_rows[t][:].rearrange("p (m u) -> p m u", u=PACK), ACT.Copy, scale=z_factor[:, t : t + 1]
+            )
+        z_q = quantise(z_grouped[:], "z")
+
+        s_banks = [psum.tile([P, V], F32, name="s_bank%d" % u, tag="bank%d" % u) for u in range(PACK)]
+        s_rows = [keep.tile([P, V], F32, name="s_rows%d" % u) for u in range(PACK)]
+        for lo, hi in QUERY_CHUNKS:
+            n = hi - lo
+            u3 = keep.tile([P, PACK, n], F32, name="u3_%d" % lo)
+            u4 = keep.tile([P, PACK, n], F32, name="u4_%d" % lo)
+            for t in range(PACK):
+                nc.vector.tensor_tensor(u3[:, t, :], b_rows[t][:].indirect(entries(n3_t, lo, hi)), own_rows[t][:, lo:hi], ALU.add)
+                nc.vector.tensor_tensor(u4[:, t, :], b_rows[t][:].indirect(entries(n4_t, lo, hi)), own_rows[t][:, lo:hi], ALU.add)
+            z2_rows = keep.tile([P, PACK, n], BF16, name="z2_rows%d" % lo)
+            nc.vector.tensor_tensor(z2_rows[:], u3[:], u4[:], ALU.max)
+            z2_grouped = keep.tile([P, PACK * n], BF16, name="z2_bf16_%d" % lo, align_bytes=64)
+            nc.scalar.copy(
+                z2_grouped[:].rearrange("p (c i t) -> p c t i", i=4, t=PACK),
+                z2_rows[:].rearrange("p t (c i) -> p c t i", i=4),
+            )
+            z2_q = quantise(z2_grouped[:], "z2_%d" % lo)
+            for u in range(PACK):
+                product(s_banks[u][:, lo:hi], z_q, u, z2_q)
+                nc.scalar.activation(s_rows[u][:, lo:hi], s_banks[u][:, lo:hi], ACT.Copy, scale=0.03125)
+
+        out_rows = out.rearrange("(p u) v -> p u v", u=PACK)
+        for u in range(PACK):
+            pieces = LAST_GATE_PIECES if u == PACK - 1 else GATE_PIECES
+            first = keep.tile([P, V], F32, name="first%d" % u)
+            diff = keep.tile([P, V], F32, name="diff%d" % u)
+            gate = keep.tile([P, V], F32, name="gate%d" % u)
+            for lo, hi in GATE_PIECES:
+                nc.vector.tensor_copy(first[:, lo:hi], s_rows[u][:].indirect(entries(n6_t, lo, hi)))
+            for lo, hi in pieces:
+                nc.vector.tensor_tensor(diff[:, lo:hi], s_rows[u][:].indirect(entries(n5_t, lo, hi)), first[:, lo:hi], ALU.subtract)
+                nc.scalar.activation(gate[:, lo:hi], diff[:, lo:hi], ACT.Tanh)
+            stores = pieces if u == PACK - 1 else ((0, V),)
+            for lo, hi in stores:
+                res = keep.tile([P, hi - lo], F32, name="res%d_%d" % (u, lo))
+                nc.vector.scalar_tensor_tensor(res[:], gate[:, lo:hi], 1.0, s_rows[u][:, lo:hi], ALU.add, ALU.mult)
+                nc.sync.dma_start(out_rows[:, u, lo:hi], res[:])

@@ -48,19 +48,19 @@ def tile_picked_kqratioovercmp_none_p_kernel(
                 halves.append(half)
             return halves
 
-        def quantise(src, name):
+        def quantise(src, name, tag=None):
             width = src.shape[1] // PACK
-            codes = keep.tile([P, width], U32, name=name + "_codes", align_bytes=64)
+            codes = keep.tile([P, width], U32, name=name + "_codes", tag=tag or name + "_codes", align_bytes=64)
             scales = keep.tile([P, width], U8, name=name + "_scales", align_bytes=64)
             nc.vector.quantize_mx(out=codes[:].bitcast(FP8X4), scales=scales[:], in_=src)
             return codes, scales
 
-        def quantise_weight(halves, name):
-            grouped = keep.tile([P, PACK * H], BF16, name=name + "_bf16", tag="grouped", align_bytes=64)
+        def quantise_weight(halves, name, grouped_tag, codes_tag):
+            grouped = keep.tile([P, PACK * H], BF16, name=name + "_bf16", tag=grouped_tag, align_bytes=64)
             dealt = grouped[:].rearrange("p (t m j) -> p m j t", t=PACK, j=PACK)
             for h, half in enumerate(halves):
                 nc.scalar.copy(dealt[:, h * (P // 2) : (h + 1) * (P // 2)], half[:].rearrange("p j (m t) -> p m j t", t=PACK))
-            return quantise(grouped[:], name)
+            return quantise(grouped[:], name, codes_tag)
 
         def product(bank, lhs, t, rhs):
             cols = slice(t * P, (t + 1) * P)
@@ -82,8 +82,8 @@ def tile_picked_kqratioovercmp_none_p_kernel(
         n2_t = load_list(n2, "n2")
         ga_t = keep.tile([P, PACK], F32, name="ga_t")
         gb_t = keep.tile([P, PACK], F32, name="gb_t")
-        nc.sync.dma_start(ga_t[:], ga.rearrange("(p t) o -> p (t o)", t=PACK))
-        nc.sync.dma_start(gb_t[:], gb.rearrange("(p t) o -> p (t o)", t=PACK))
+        nc.gpsimd.dma_start(ga_t[:], ga.rearrange("(p t) o -> p (t o)", t=PACK))
+        nc.gpsimd.dma_start(gb_t[:], gb.rearrange("(p t) o -> p (t o)", t=PACK))
         w2_raw = load_weight(w2, "w2")
         n3_t = load_list(n3, "n3")
         n4_t = load_list(n4, "n4")
@@ -91,7 +91,7 @@ def tile_picked_kqratioovercmp_none_p_kernel(
         n6_t = load_list(n6, "n6")
 
         half_col = keep.tile([P, 1], F32, name="half_col")
-        nc.vector.memset(half_col[:], 0.5)
+        nc.gpsimd.memset(half_col[:], 0.5)
 
         def pick(table, dtype, offsets, name):
             picked = keep.tile([P, S], dtype, name=name, align_bytes=64)
@@ -100,7 +100,7 @@ def tile_picked_kqratioovercmp_none_p_kernel(
 
         a_bytes = pick(byte_table[:], U8, offs_t, "a_bytes")
         b_bytes = pick(byte_table[:], U8, two_t, "b_bytes")
-        w1_q = quantise_weight(w1_raw, "w1")
+        w1_q = quantise_weight(w1_raw, "w1", "w1_bf16", "grouped")
         a_words = pick(word_table[:].bitcast(U32), U32, offs_t, "a_words")
         b_words = pick(word_table[:].bitcast(U32), U32, two_t, "b_words")
 
@@ -112,50 +112,39 @@ def tile_picked_kqratioovercmp_none_p_kernel(
             nc.scalar.copy(rows[:], bank[:])
             a_rows.append(rows)
 
+        twice_positive = keep.tile([P, PACK], F32, name="twice_positive")
+        nc.gpsimd.tensor_scalar(twice_positive[:], gb_t[:], 0.0, 2.0, ALU.is_ge, ALU.mult)
         sign_b = keep.tile([P, PACK], F32, name="sign_b")
-        nc.vector.tensor_scalar(sign_b[:], gb_t[:], 0.0, 2.0, ALU.is_ge, ALU.mult)
+        nc.gpsimd.tensor_scalar(sign_b[:], twice_positive[:], 1.0, -1.0, ALU.mult, ALU.add)
         z_factor = keep.tile([P, PACK], F32, name="z_factor")
-        nc.vector.scalar_tensor_tensor(z_factor[:], sign_b[:], -1.0, ga_t[:], ALU.add, ALU.mult)
+        nc.gpsimd.tensor_tensor(z_factor[:], sign_b[:], ga_t[:], ALU.mult)
         b_factor = keep.tile([P, PACK], F32, name="b_factor")
-        nc.vector.scalar_tensor_tensor(b_factor[:], sign_b[:], -1.0, gb_t[:], ALU.add, ALU.mult)
+        nc.gpsimd.tensor_tensor(b_factor[:], sign_b[:], gb_t[:], ALU.mult)
         own_factor = keep.tile([P, PACK], F32, name="own_factor")
-        nc.vector.tensor_scalar(own_factor[:], b_factor[:], -0.75, None, ALU.mult)
+        nc.gpsimd.tensor_scalar(own_factor[:], b_factor[:], -0.75, 0.0, ALU.mult, ALU.add)
+
+        w2_q = quantise_weight(w2_raw, "w2", "grouped", None)
 
         pa = keep.tile([P, PACK, W], F32, name="pa")
         pb = keep.tile([P, PACK, W], F32, name="pb")
-        rb = keep.tile([P, PACK, W], F32, name="rb")
-        size_b = keep.tile([P, PACK, W], F32, name="size_b")
+        size_b = keep.tile([P, PACK, W], F32, name="size_b", tag="w2_raw1")
         root = keep.tile([P, PACK, W], F32, name="root")
         inverse = keep.tile([P, PACK, W], F32, name="inverse")
         dt_rows = [keep.tile([P, S], F32, name="dt_rows%d" % t) for t in range(PACK)]
-
-        def fetch_pairs(t):
+        for t in range(PACK):
             nc.vector.tensor_copy(pb[:, t, :], a_rows[t][:].indirect(n2_t[:]))
             nc.vector.tensor_copy(pa[:, t, :], a_rows[t][:].indirect(n1_t[:]))
-            nc.scalar.activation(size_b[:, t, :], pb[:, t, :], ACT.Abs)
-            nc.scalar.activation(root[:, t, :], size_b[:, t, :], ACT.Abs_reciprocal_sqrt, bias=half_col[:])
-            nc.scalar.activation(inverse[:, t, :], root[:, t, :], ACT.Square)
-
-        def put_larger(t):
-            nc.vector.tensor_tensor(rb[:, t, :], pa[:, t, :], pb[:, t, :], ALU.max)
-
-        def scatter_b(t):
+        nc.scalar.activation(size_b[:], pb[:], ACT.Abs)
+        nc.scalar.activation(root[:], size_b[:], ACT.Abs_reciprocal_sqrt, bias=half_col[:])
+        nc.scalar.activation(inverse[:], root[:], ACT.Square)
+        rb = keep.tile([P, PACK, W], F32, name="rb", tag="grouped", align_bytes=64)
+        for h in range(2):
+            nc.vector.tensor_tensor(rb[:, 2 * h : 2 * h + 2], pa[:, 2 * h : 2 * h + 2], pb[:, 2 * h : 2 * h + 2], ALU.max)
+        for t in range(PACK):
             nc.vector.tensor_copy(dt_rows[t][:].indirect(n2_t[:]), rb[:, t, :])
-
-        def scatter_a(t):
+        for t in range(PACK):
             nc.vector.tensor_tensor(dt_rows[t][:].indirect(n1_t[:]), pa[:, t, :], inverse[:, t, :], ALU.mult)
 
-        fetch_pairs(0)
-        for t in range(PACK):
-            if t + 1 < PACK:
-                fetch_pairs(t + 1)
-            put_larger(t)
-            if t > 0:
-                scatter_a(t - 1)
-            scatter_b(t)
-
-        w2_q = quantise_weight(w2_raw, "w2")
-        scatter_a(PACK - 1)
         b_rows, own_rows = [], []
         for t in range(PACK):
             bank = psum.tile([P, V], F32, name="b_bank%d" % t, tag="bank%d" % (PACK + t))
@@ -179,8 +168,8 @@ def tile_picked_kqratioovercmp_none_p_kernel(
         s_rows = [keep.tile([P, V], F32, name="s_rows%d" % u) for u in range(PACK)]
         for lo, hi in QUERY_CHUNKS:
             n = hi - lo
-            u3 = keep.tile([P, PACK, n], F32, name="u3_%d" % lo)
-            u4 = keep.tile([P, PACK, n], F32, name="u4_%d" % lo)
+            u3 = keep.tile([P, PACK, n], F32, name="u3_%d" % lo, tag="u3")
+            u4 = keep.tile([P, PACK, n], F32, name="u4_%d" % lo, tag="u4")
             for t in range(PACK):
                 nc.vector.tensor_tensor(u3[:, t, :], b_rows[t][:].indirect(entries(n3_t, lo, hi)), own_rows[t][:, lo:hi], ALU.add)
                 nc.vector.tensor_tensor(u4[:, t, :], b_rows[t][:].indirect(entries(n4_t, lo, hi)), own_rows[t][:, lo:hi], ALU.add)

@@ -14,12 +14,15 @@ ACT = mybir.ActivationFunctionType
 
 P = 128
 PACK = 4
+QUADRANT = 32
+LIST_COLUMN = 16
+RUN = 4
+MX_ALIGN = 64
 K, T, S, V, H, W = 512, 2048, 512, 512, 512, 256
-LIST_COL = 16
-FLOPS = 3 * 2 * 512 * 512 * 512
+FLOPS = 2 * K * H * S + 2 * K * H * V + 2 * H * S * V
 
 QUERY_CHUNKS = ((0, 256), (256, 384), (384, 512))
-GATE_PIECES = ((0, 256), (256, 512))
+GATE_HALVES = ((0, 256), (256, 512))
 LAST_GATE_PIECES = ((0, 256), (256, 384), (384, 512))
 
 
@@ -37,8 +40,8 @@ def tile_picked_kqratioovercmp_none_p_kernel(
             nc.sync.dma_start(tile[:], src)
             return tile
 
-        def entries(tile, lo, hi):
-            return tile[:, lo // LIST_COL : hi // LIST_COL]
+        def entries(list_tile, lo, hi):
+            return list_tile[:, lo // LIST_COLUMN : hi // LIST_COLUMN]
 
         def load_weight(w, name):
             halves = []
@@ -48,38 +51,45 @@ def tile_picked_kqratioovercmp_none_p_kernel(
                 halves.append(half)
             return halves
 
-        def quantise(src, name, tag=None):
-            width = src.shape[1] // PACK
-            codes = keep.tile([P, width], U32, name=name + "_codes", tag=tag or name + "_codes", align_bytes=64)
-            scales = keep.tile([P, width], U8, name=name + "_scales", align_bytes=64)
-            nc.vector.quantize_mx(out=codes[:].bitcast(FP8X4), scales=scales[:], in_=src)
-            return codes, scales
+        def quantise(woven, name, words_tag=None):
+            width = woven.shape[1] // PACK
+            words = keep.tile([P, width], U32, name=name + "_words", tag=words_tag or name + "_words", align_bytes=MX_ALIGN)
+            scales = keep.tile([P, width], U8, name=name + "_scales", align_bytes=MX_ALIGN)
+            nc.vector.quantize_mx(out=words[:].bitcast(FP8X4), scales=scales[:], in_=woven)
+            return words, scales
 
-        def quantise_weight(halves, name, grouped_tag, codes_tag):
-            grouped = keep.tile([P, PACK * H], BF16, name=name + "_bf16", tag=grouped_tag, align_bytes=64)
-            dealt = grouped[:].rearrange("p (t m j) -> p m j t", t=PACK, j=PACK)
+        def quantise_weight(halves, name, woven_tag, words_tag):
+            woven = keep.tile([P, PACK * H], BF16, name=name + "_woven", tag=woven_tag, align_bytes=MX_ALIGN)
+            dealt = woven[:].rearrange("p (t m j) -> p m j t", t=PACK, j=PACK)
             for h, half in enumerate(halves):
                 nc.scalar.copy(dealt[:, h * (P // 2) : (h + 1) * (P // 2)], half[:].rearrange("p j (m t) -> p m j t", t=PACK))
-            return quantise(grouped[:], name, codes_tag)
+            return quantise(woven[:], name, words_tag)
 
-        def product(bank, lhs, t, rhs):
-            cols = slice(t * P, (t + 1) * P)
+        def product(result, stationary, block, moving):
+            cols = slice(block * P, (block + 1) * P)
             nc.tensor.matmul_mx(
-                out=bank, lhsT=lhs[0][:, cols].bitcast(FP8X4), lhsT_scale=lhs[1][:, cols],
-                rhs=rhs[0][:].bitcast(FP8X4), rhs_scale=rhs[1][:], start=True, stop=True,
+                out=result,
+                lhsT=stationary[0][:, cols].bitcast(FP8X4),
+                lhsT_scale=stationary[1][:, cols],
+                rhs=moving[0][:].bitcast(FP8X4),
+                rhs_scale=moving[1][:],
+                start=True,
+                stop=True,
             )
 
         byte_table = keep.tile([P, T], U8, name="byte_table")
         nc.vector.memset(byte_table[:].bitcast(I32), 0)
         offs_t = load_list(offs, "offs")
-        two_t = load_list(two, "two")
-        for q in range(4):
-            nc.scalar.dma_start(byte_table[32 * q : 32 * q + 4, :].bitcast(I32), x_scales[0, 4 * q : 4 * q + 4, :].bitcast(I32))
+        n2_t = load_list(n2, "n2")
+        for q in range(P // QUADRANT):
+            nc.scalar.dma_start(
+                byte_table[QUADRANT * q : QUADRANT * q + 4, :].bitcast(I32), x_scales[0, 4 * q : 4 * q + 4, :].bitcast(I32)
+            )
         w1_raw = load_weight(w1, "w1")
         word_table = keep.tile([P, T], I32, name="word_table")
         nc.sync.dma_start(word_table[:], x_words[0].rearrange("p c r -> p (c r)").bitcast(I32))
+        two_t = load_list(two, "two")
         n1_t = load_list(n1, "n1")
-        n2_t = load_list(n2, "n2")
         ga_t = keep.tile([P, PACK], F32, name="ga_t")
         gb_t = keep.tile([P, PACK], F32, name="gb_t")
         nc.gpsimd.dma_start(ga_t[:], ga.rearrange("(p t) o -> p (t o)", t=PACK))
@@ -90,54 +100,54 @@ def tile_picked_kqratioovercmp_none_p_kernel(
         n5_t = load_list(n5, "n5")
         n6_t = load_list(n6, "n6")
 
-        half_col = keep.tile([P, 1], F32, name="half_col")
-        nc.gpsimd.memset(half_col[:], 0.5)
+        half_bias = keep.tile([P, 1], F32, name="half_bias")
+        nc.gpsimd.memset(half_bias[:], 0.5)
 
-        def pick(table, dtype, offsets, name):
-            picked = keep.tile([P, S], dtype, name=name, align_bytes=64)
-            nc.vector.tensor_copy(picked[:], table.indirect(offsets[:]))
+        def pick(table, dtype, list_tile, name):
+            picked = keep.tile([P, S], dtype, name=name, align_bytes=MX_ALIGN)
+            nc.vector.tensor_copy(picked[:], table.indirect(list_tile[:]))
             return picked
 
-        a_bytes = pick(byte_table[:], U8, offs_t, "a_bytes")
-        b_bytes = pick(byte_table[:], U8, two_t, "b_bytes")
-        w1_q = quantise_weight(w1_raw, "w1", "w1_bf16", "grouped")
-        a_words = pick(word_table[:].bitcast(U32), U32, offs_t, "a_words")
-        b_words = pick(word_table[:].bitcast(U32), U32, two_t, "b_words")
+        xa_bytes = pick(byte_table[:], U8, offs_t, "xa_bytes")
+        w1_mx = quantise_weight(w1_raw, "w1", "w1_woven", "stage")
+        xa_words = pick(word_table[:].bitcast(U32), U32, offs_t, "xa_words")
+        xb_words = pick(word_table[:].bitcast(U32), U32, two_t, "xb_words")
+        xb_bytes = pick(byte_table[:], U8, two_t, "xb_bytes")
 
         a_rows = []
         for t in range(PACK):
             bank = psum.tile([P, S], F32, name="a_bank%d" % t, tag="bank%d" % t)
-            product(bank[:], w1_q, t, (a_words, a_bytes))
+            product(bank[:], w1_mx, t, (xa_words, xa_bytes))
             rows = keep.tile([P, S], F32, name="a_rows%d" % t)
             nc.scalar.copy(rows[:], bank[:])
             a_rows.append(rows)
 
         twice_positive = keep.tile([P, PACK], F32, name="twice_positive")
         nc.gpsimd.tensor_scalar(twice_positive[:], gb_t[:], 0.0, 2.0, ALU.is_ge, ALU.mult)
-        sign_b = keep.tile([P, PACK], F32, name="sign_b")
-        nc.gpsimd.tensor_scalar(sign_b[:], twice_positive[:], 1.0, -1.0, ALU.mult, ALU.add)
+        gb_sign = keep.tile([P, PACK], F32, name="gb_sign")
+        nc.gpsimd.tensor_scalar(gb_sign[:], twice_positive[:], 1.0, -1.0, ALU.mult, ALU.add)
         z_factor = keep.tile([P, PACK], F32, name="z_factor")
-        nc.gpsimd.tensor_tensor(z_factor[:], sign_b[:], ga_t[:], ALU.mult)
+        nc.gpsimd.tensor_tensor(z_factor[:], gb_sign[:], ga_t[:], ALU.mult)
         b_factor = keep.tile([P, PACK], F32, name="b_factor")
-        nc.gpsimd.tensor_tensor(b_factor[:], sign_b[:], gb_t[:], ALU.mult)
+        nc.gpsimd.tensor_tensor(b_factor[:], gb_sign[:], gb_t[:], ALU.mult)
         own_factor = keep.tile([P, PACK], F32, name="own_factor")
         nc.gpsimd.tensor_scalar(own_factor[:], b_factor[:], -0.75, 0.0, ALU.mult, ALU.add)
 
-        w2_q = quantise_weight(w2_raw, "w2", "grouped", None)
+        w2_mx = quantise_weight(w2_raw, "w2", "stage", None)
 
         pa = keep.tile([P, PACK, W], F32, name="pa")
         pb = keep.tile([P, PACK, W], F32, name="pb")
-        size_b = keep.tile([P, PACK, W], F32, name="size_b", tag="w2_raw1")
-        root = keep.tile([P, PACK, W], F32, name="root")
+        pb_size = keep.tile([P, PACK, W], F32, name="pb_size", tag="w2_raw1")
+        inverse_root = keep.tile([P, PACK, W], F32, name="inverse_root")
         inverse = keep.tile([P, PACK, W], F32, name="inverse")
         dt_rows = [keep.tile([P, S], F32, name="dt_rows%d" % t) for t in range(PACK)]
         for t in range(PACK):
             nc.vector.tensor_copy(pb[:, t, :], a_rows[t][:].indirect(n2_t[:]))
             nc.vector.tensor_copy(pa[:, t, :], a_rows[t][:].indirect(n1_t[:]))
-        nc.scalar.activation(size_b[:], pb[:], ACT.Abs)
-        nc.scalar.activation(root[:], size_b[:], ACT.Abs_reciprocal_sqrt, bias=half_col[:])
-        nc.scalar.activation(inverse[:], root[:], ACT.Square)
-        rb = keep.tile([P, PACK, W], F32, name="rb", tag="grouped", align_bytes=64)
+        nc.scalar.activation(pb_size[:], pb[:], ACT.Abs)
+        nc.scalar.activation(inverse_root[:], pb_size[:], ACT.Abs_reciprocal_sqrt, bias=half_bias[:])
+        nc.scalar.activation(inverse[:], inverse_root[:], ACT.Square)
+        rb = keep.tile([P, PACK, W], F32, name="rb", tag="stage", align_bytes=MX_ALIGN)
         for h in range(2):
             nc.vector.tensor_tensor(rb[:, 2 * h : 2 * h + 2], pa[:, 2 * h : 2 * h + 2], pb[:, 2 * h : 2 * h + 2], ALU.max)
         for t in range(PACK):
@@ -148,7 +158,7 @@ def tile_picked_kqratioovercmp_none_p_kernel(
         b_rows, own_rows = [], []
         for t in range(PACK):
             bank = psum.tile([P, V], F32, name="b_bank%d" % t, tag="bank%d" % (PACK + t))
-            product(bank[:], w2_q, t, (b_words, b_bytes))
+            product(bank[:], w2_mx, t, (xb_words, xb_bytes))
             rows = keep.tile([P, V], F32, name="b_rows%d" % t)
             nc.scalar.activation(rows[:], bank[:], ACT.Copy, scale=b_factor[:, t : t + 1])
             own = keep.tile([P, V], F32, name="own_rows%d" % t)
@@ -156,48 +166,69 @@ def tile_picked_kqratioovercmp_none_p_kernel(
             b_rows.append(rows)
             own_rows.append(own)
 
-        z_grouped = keep.tile([P, PACK * S], BF16, name="z_bf16", tag="grouped", align_bytes=64)
-        z_dealt = z_grouped[:].rearrange("p (u m t) -> p t m u", u=PACK, t=PACK)
+        z_woven = keep.tile([P, PACK * S], BF16, name="z_woven", tag="stage", align_bytes=MX_ALIGN)
+        z_dealt = z_woven[:].rearrange("p (u m t) -> p t m u", u=PACK, t=PACK)
         for t in range(PACK):
             nc.scalar.activation(
                 z_dealt[:, t], dt_rows[t][:].rearrange("p (m u) -> p m u", u=PACK), ACT.Copy, scale=z_factor[:, t : t + 1]
             )
-        z_q = quantise(z_grouped[:], "z")
+        z_first = quantise(z_woven[:, : PACK * P], "z_first")
 
         s_banks = [psum.tile([P, V], F32, name="s_bank%d" % u, tag="bank%d" % u) for u in range(PACK)]
-        s_rows = [keep.tile([P, V], F32, name="s_rows%d" % u) for u in range(PACK)]
+        half_s_rows = [keep.tile([P, V], F32, name="half_s_rows%d" % u) for u in range(PACK)]
+        half_s_scale = 0.0625 / 2
+        z2_chunks = []
         for lo, hi in QUERY_CHUNKS:
             n = hi - lo
-            u3 = keep.tile([P, PACK, n], F32, name="u3_%d" % lo, tag="u3")
-            u4 = keep.tile([P, PACK, n], F32, name="u4_%d" % lo, tag="u4")
+            is_last = hi == V
+            at_n3 = keep.tile([P, PACK, n], F32, name="at_n3_%d" % lo, tag="at_n3", align_bytes=MX_ALIGN)
+            at_n4 = keep.tile([P, PACK, n], F32, name="at_n4_%d" % lo, tag="first_woven" if is_last else "at_n4", align_bytes=MX_ALIGN)
             for t in range(PACK):
-                nc.vector.tensor_tensor(u3[:, t, :], b_rows[t][:].indirect(entries(n3_t, lo, hi)), own_rows[t][:, lo:hi], ALU.add)
-                nc.vector.tensor_tensor(u4[:, t, :], b_rows[t][:].indirect(entries(n4_t, lo, hi)), own_rows[t][:, lo:hi], ALU.add)
-            z2_rows = keep.tile([P, PACK, n], BF16, name="z2_rows%d" % lo)
-            nc.vector.tensor_tensor(z2_rows[:], u3[:], u4[:], ALU.max)
-            z2_grouped = keep.tile([P, PACK * n], BF16, name="z2_bf16_%d" % lo, align_bytes=64)
-            nc.scalar.copy(
-                z2_grouped[:].rearrange("p (c i t) -> p c t i", i=4, t=PACK),
-                z2_rows[:].rearrange("p t (c i) -> p c t i", i=4),
+                own = own_rows[t][:, lo:hi]
+                nc.vector.tensor_tensor(at_n3[:, t, :], b_rows[t][:].indirect(entries(n3_t, lo, hi)), own, ALU.add)
+                nc.vector.tensor_tensor(at_n4[:, t, :], b_rows[t][:].indirect(entries(n4_t, lo, hi)), own, ALU.add)
+            z2_woven = keep.tile(
+                [P, PACK * n], BF16, name="z2_woven%d" % lo, tag="first_woven" if lo == 0 else "later_woven", align_bytes=MX_ALIGN
             )
-            z2_q = quantise(z2_grouped[:], "z2_%d" % lo)
-            for u in range(PACK):
-                product(s_banks[u][:, lo:hi], z_q, u, z2_q)
-                nc.scalar.activation(s_rows[u][:, lo:hi], s_banks[u][:, lo:hi], ACT.Copy, scale=0.03125)
+            by_runs = z2_woven[:].rearrange("p (c i t) -> p c t i", i=RUN, t=PACK)
+            if is_last:
+                nc.vector.tensor_tensor(
+                    by_runs,
+                    at_n3[:].rearrange("p t (c i) -> p c t i", i=RUN),
+                    at_n4[:].rearrange("p t (c i) -> p c t i", i=RUN),
+                    ALU.max,
+                )
+            else:
+                z2_rows = keep.tile([P, PACK, n], BF16, name="z2_rows%d" % lo)
+                nc.vector.tensor_tensor(z2_rows[:], at_n3[:], at_n4[:], ALU.max)
+                nc.scalar.copy(by_runs, z2_rows[:].rearrange("p t (c i) -> p c t i", i=RUN))
+            z2_mx = quantise(z2_woven[:], "z2_%d" % lo)
+            z2_chunks.append(z2_mx)
+            product(s_banks[0][:, lo:hi], z_first, 0, z2_mx)
+            nc.scalar.activation(half_s_rows[0][:, lo:hi], s_banks[0][:, lo:hi], ACT.Copy, scale=half_s_scale)
+
+        z_second = quantise(z_woven[:, PACK * P : 2 * PACK * P], "z_second", "at_n3")
+        z_rest = quantise(z_woven[:, 2 * PACK * P :], "z_rest", "first_woven")
+        for u, (z_mx, block) in ((1, (z_second, 0)), (2, (z_rest, 0)), (3, (z_rest, 1))):
+            for (lo, hi), z2_mx in zip(QUERY_CHUNKS, z2_chunks):
+                product(s_banks[u][:, lo:hi], z_mx, block, z2_mx)
+            nc.scalar.activation(half_s_rows[u][:], s_banks[u][:], ACT.Copy, scale=half_s_scale)
 
         out_rows = out.rearrange("(p u) v -> p u v", u=PACK)
         for u in range(PACK):
-            pieces = LAST_GATE_PIECES if u == PACK - 1 else GATE_PIECES
-            first = keep.tile([P, V], F32, name="first%d" % u)
-            diff = keep.tile([P, V], F32, name="diff%d" % u)
-            gate = keep.tile([P, V], F32, name="gate%d" % u)
-            for lo, hi in GATE_PIECES:
-                nc.vector.tensor_copy(first[:, lo:hi], s_rows[u][:].indirect(entries(n6_t, lo, hi)))
+            is_last = u == PACK - 1
+            pieces = LAST_GATE_PIECES if is_last else GATE_HALVES
+            at_n6 = keep.tile([P, V], F32, name="at_n6_%d" % u)
+            half_diff = keep.tile([P, V], F32, name="half_diff%d" % u, tag="tanh%d" % (u - 1) if is_last else "half_diff%d" % u)
+            tanh_rows = keep.tile([P, V], F32, name="tanh%d" % u)
+            for lo, hi in GATE_HALVES:
+                nc.vector.tensor_copy(at_n6[:, lo:hi], half_s_rows[u][:].indirect(entries(n6_t, lo, hi)))
             for lo, hi in pieces:
-                nc.vector.tensor_tensor(diff[:, lo:hi], s_rows[u][:].indirect(entries(n5_t, lo, hi)), first[:, lo:hi], ALU.subtract)
-                nc.scalar.activation(gate[:, lo:hi], diff[:, lo:hi], ACT.Tanh)
-            stores = pieces if u == PACK - 1 else ((0, V),)
-            for lo, hi in stores:
-                res = keep.tile([P, hi - lo], F32, name="res%d_%d" % (u, lo))
-                nc.vector.scalar_tensor_tensor(res[:], gate[:, lo:hi], 1.0, s_rows[u][:, lo:hi], ALU.add, ALU.mult)
-                nc.sync.dma_start(out_rows[:, u, lo:hi], res[:])
+                nc.vector.tensor_tensor(
+                    half_diff[:, lo:hi], half_s_rows[u][:].indirect(entries(n5_t, lo, hi)), at_n6[:, lo:hi], ALU.subtract
+                )
+                nc.scalar.activation(tanh_rows[:, lo:hi], half_diff[:, lo:hi], ACT.Tanh)
+            for lo, hi in pieces if is_last else ((0, V),):
+                gated = keep.tile([P, hi - lo], F32, name="gated%d_%d" % (u, lo))
+                nc.vector.scalar_tensor_tensor(gated[:], tanh_rows[:, lo:hi], 1.0, half_s_rows[u][:, lo:hi], ALU.add, ALU.mult)
+                nc.sync.dma_start(out_rows[:, u, lo:hi], gated[:])

from contextlib import ExitStack

import concourse.mybir as mybir

F32 = mybir.dt.float32
BF16 = mybir.dt.bfloat16
U32 = mybir.dt.uint32
I32 = mybir.dt.int32
U16 = mybir.dt.uint16
U8 = mybir.dt.uint8
FP8X4 = mybir.dt.float8_e4m3fn_x4
ALU = mybir.AluOpType
ACT = mybir.ActivationFunctionType

P = 128
PACK = 4
QUADRANT = 32
LIST_COLUMN = 16
RUN = 4
MX_ALIGN = 64
K, T, S, V, H, W = 512, 2048, 512, 512, 512, 256
FLOPS = 2 * K * H * S + 2 * K * H * V + 2 * H * S * V

QUERY_CHUNKS = ((0, 256), (256, 384), (384, 512))
GATE_HALVES = ((0, 256), (256, 512))
LAST_GATE_PIECES = ((0, 256), (256, 384), (384, 512))


def tile_picked_kqratioovercmp_none_p_kernel(
    tc, x_words, x_scales, w1, w2, ga, gb, offs, two, n1, n2, n3, n4, n5, n6, out
):
    nc = tc.nc
    with ExitStack() as ctx:
        lists = ctx.enter_context(tc.tile_pool(name="lists", bufs=1))
        keep = ctx.enter_context(tc.tile_pool(name="keep", bufs=1))
        psum = ctx.enter_context(tc.psum_pool(name="psum", bufs=1))

        def load_list(src, name):
            tile = lists.tile(list(src.shape), U16, name=name)
            nc.sync.dma_start(tile[:], src)
            return tile

        def entries(list_tile, lo, hi):
            return list_tile[:, lo // LIST_COLUMN : hi // LIST_COLUMN]

        def load_weight(w, name):
            halves = []
            for h in range(2):
                half = keep.tile([P, PACK, H // 2], F32, name="%s_raw%d" % (name, h))
                nc.sync.dma_start(half[:], w.rearrange("(p j) c -> p j c", j=PACK)[:, :, h * (H // 2) : (h + 1) * (H // 2)])
                halves.append(half)
            return halves

        def quantise(woven, name, words_tag=None):
            width = woven.shape[1] // PACK
            words = keep.tile([P, width], U32, name=name + "_words", tag=words_tag or name + "_words", align_bytes=MX_ALIGN)
            scales = keep.tile([P, width], U8, name=name + "_scales", align_bytes=MX_ALIGN)
            nc.vector.quantize_mx(out=words[:].bitcast(FP8X4), scales=scales[:], in_=woven)
            return words, scales

        def quantise_weight(halves, name, woven_tag, words_tag):
            woven = keep.tile([P, PACK * H], BF16, name=name + "_woven", tag=woven_tag, align_bytes=MX_ALIGN)
            dealt = woven[:].rearrange("p (t m j) -> p m j t", t=PACK, j=PACK)
            for h, half in enumerate(halves):
                nc.scalar.copy(dealt[:, h * (P // 2) : (h + 1) * (P // 2)], half[:].rearrange("p j (m t) -> p m j t", t=PACK))
            return quantise(woven[:], name, words_tag)

        def product(result, stationary, block, moving):
            cols = slice(block * P, (block + 1) * P)
            nc.tensor.matmul_mx(
                out=result,
                lhsT=stationary[0][:, cols].bitcast(FP8X4),
                lhsT_scale=stationary[1][:, cols],
                rhs=moving[0][:].bitcast(FP8X4),
                rhs_scale=moving[1][:],
                start=True,
                stop=True,
            )

        byte_table = keep.tile([P, T], U8, name="byte_table")
        nc.vector.memset(byte_table[:].bitcast(I32), 0)
        offs_t = load_list(offs, "offs")
        n2_t = load_list(n2, "n2")
        for q in range(P // QUADRANT):
            nc.scalar.dma_start(
                byte_table[QUADRANT * q : QUADRANT * q + 4, :].bitcast(I32), x_scales[0, 4 * q : 4 * q + 4, :].bitcast(I32)
            )
        w1_raw = load_weight(w1, "w1")
        word_table = keep.tile([P, T], I32, name="word_table")
        nc.sync.dma_start(word_table[:], x_words[0].rearrange("p c r -> p (c r)").bitcast(I32))
        two_t = load_list(two, "two")
        n1_t = load_list(n1, "n1")
        ga_t = keep.tile([P, PACK], F32, name="ga_t")
        gb_t = keep.tile([P, PACK], F32, name="gb_t")
        nc.gpsimd.dma_start(ga_t[:], ga.rearrange("(p t) o -> p (t o)", t=PACK))
        nc.gpsimd.dma_start(gb_t[:], gb.rearrange("(p t) o -> p (t o)", t=PACK))
        w2_raw = load_weight(w2, "w2")
        n3_t = load_list(n3, "n3")
        n4_t = load_list(n4, "n4")
        n5_t = load_list(n5, "n5")
        n6_t = load_list(n6, "n6")

        half_bias = keep.tile([P, 1], F32, name="half_bias")
        nc.gpsimd.memset(half_bias[:], 0.5)

        def pick(table, dtype, list_tile, name):
            picked = keep.tile([P, S], dtype, name=name, align_bytes=MX_ALIGN)
            nc.vector.tensor_copy(picked[:], table.indirect(list_tile[:]))
            return picked

        xa_bytes = pick(byte_table[:], U8, offs_t, "xa_bytes")
        w1_mx = quantise_weight(w1_raw, "w1", "w1_woven", "stage")
        xa_words = pick(word_table[:].bitcast(U32), U32, offs_t, "xa_words")
        xb_words = pick(word_table[:].bitcast(U32), U32, two_t, "xb_words")
        xb_bytes = pick(byte_table[:], U8, two_t, "xb_bytes")

        a_rows = []
        for t in range(PACK):
            bank = psum.tile([P, S], F32, name="a_bank%d" % t, tag="bank%d" % t)
            product(bank[:], w1_mx, t, (xa_words, xa_bytes))
            rows = keep.tile([P, S], F32, name="a_rows%d" % t)
            nc.scalar.copy(rows[:], bank[:])
            a_rows.append(rows)

        twice_positive = keep.tile([P, PACK], F32, name="twice_positive")
        nc.gpsimd.tensor_scalar(twice_positive[:], gb_t[:], 0.0, 2.0, ALU.is_ge, ALU.mult)
        gb_sign = keep.tile([P, PACK], F32, name="gb_sign")
        nc.gpsimd.tensor_scalar(gb_sign[:], twice_positive[:], 1.0, -1.0, ALU.mult, ALU.add)
        z_factor = keep.tile([P, PACK], F32, name="z_factor")
        nc.gpsimd.tensor_tensor(z_factor[:], gb_sign[:], ga_t[:], ALU.mult)
        b_factor = keep.tile([P, PACK], F32, name="b_factor")
        nc.gpsimd.tensor_tensor(b_factor[:], gb_sign[:], gb_t[:], ALU.mult)
        own_factor = keep.tile([P, PACK], F32, name="own_factor")
        nc.gpsimd.tensor_scalar(own_factor[:], b_factor[:], -0.75, 0.0, ALU.mult, ALU.add)

        w2_mx = quantise_weight(w2_raw, "w2", "stage", None)

        pa = keep.tile([P, PACK, W], F32, name="pa")
        pb = keep.tile([P, PACK, W], F32, name="pb")
        pb_size = keep.tile([P, PACK, W], F32, name="pb_size", tag="w2_raw1")
        inverse_root = keep.tile([P, PACK, W], F32, name="inverse_root")
        inverse = keep.tile([P, PACK, W], F32, name="inverse")
        dt_rows = [keep.tile([P, S], F32, name="dt_rows%d" % t) for t in range(PACK)]
        for t in range(PACK):
            nc.vector.tensor_copy(pb[:, t, :], a_rows[t][:].indirect(n2_t[:]))
            nc.vector.tensor_copy(pa[:, t, :], a_rows[t][:].indirect(n1_t[:]))
        nc.scalar.activation(pb_size[:], pb[:], ACT.Abs)
        nc.scalar.activation(inverse_root[:], pb_size[:], ACT.Abs_reciprocal_sqrt, bias=half_bias[:])
        nc.scalar.activation(inverse[:], inverse_root[:], ACT.Square)
        rb = keep.tile([P, PACK, W], F32, name="rb", tag="stage", align_bytes=MX_ALIGN)
        for h in range(2):
            nc.vector.tensor_tensor(rb[:, 2 * h : 2 * h + 2], pa[:, 2 * h : 2 * h + 2], pb[:, 2 * h : 2 * h + 2], ALU.max)
        for t in range(PACK):
            nc.vector.tensor_copy(dt_rows[t][:].indirect(n2_t[:]), rb[:, t, :])
        for t in range(PACK):
            nc.vector.tensor_tensor(dt_rows[t][:].indirect(n1_t[:]), pa[:, t, :], inverse[:, t, :], ALU.mult)

        b_rows, own_rows = [], []
        for t in range(PACK):
            bank = psum.tile([P, V], F32, name="b_bank%d" % t, tag="bank%d" % (PACK + t))
            product(bank[:], w2_mx, t, (xb_words, xb_bytes))
            rows = keep.tile([P, V], F32, name="b_rows%d" % t)
            nc.scalar.activation(rows[:], bank[:], ACT.Copy, scale=b_factor[:, t : t + 1])
            own = keep.tile([P, V], F32, name="own_rows%d" % t)
            nc.scalar.activation(own[:], bank[:], ACT.Copy, scale=own_factor[:, t : t + 1])
            b_rows.append(rows)
            own_rows.append(own)

        z_woven = keep.tile([P, PACK * S], BF16, name="z_woven", tag="stage", align_bytes=MX_ALIGN)
        z_dealt = z_woven[:].rearrange("p (u m t) -> p t m u", u=PACK, t=PACK)
        for t in range(PACK):
            nc.scalar.activation(
                z_dealt[:, t], dt_rows[t][:].rearrange("p (m u) -> p m u", u=PACK), ACT.Copy, scale=z_factor[:, t : t + 1]
            )
        z_first = quantise(z_woven[:, : PACK * P], "z_first")

        s_banks = [psum.tile([P, V], F32, name="s_bank%d" % u, tag="bank%d" % u) for u in range(PACK)]
        half_s_rows = [keep.tile([P, V], F32, name="half_s_rows%d" % u) for u in range(PACK)]
        half_s_scale = 0.0625 / 2
        z2_chunks = []
        for lo, hi in QUERY_CHUNKS:
            n = hi - lo
            is_last = hi == V
            at_n3 = keep.tile([P, PACK, n], F32, name="at_n3_%d" % lo, tag="at_n3", align_bytes=MX_ALIGN)
            at_n4 = keep.tile([P, PACK, n], F32, name="at_n4_%d" % lo, tag="first_woven" if is_last else "at_n4", align_bytes=MX_ALIGN)
            for t in range(PACK):
                own = own_rows[t][:, lo:hi]
                nc.vector.tensor_tensor(at_n3[:, t, :], b_rows[t][:].indirect(entries(n3_t, lo, hi)), own, ALU.add)
                nc.vector.tensor_tensor(at_n4[:, t, :], b_rows[t][:].indirect(entries(n4_t, lo, hi)), own, ALU.add)
            z2_woven = keep.tile(
                [P, PACK * n], BF16, name="z2_woven%d" % lo, tag="first_woven" if lo == 0 else "later_woven", align_bytes=MX_ALIGN
            )
            by_runs = z2_woven[:].rearrange("p (c i t) -> p c t i", i=RUN, t=PACK)
            if is_last:
                nc.vector.tensor_tensor(
                    by_runs,
                    at_n3[:].rearrange("p t (c i) -> p c t i", i=RUN),
                    at_n4[:].rearrange("p t (c i) -> p c t i", i=RUN),
                    ALU.max,
                )
            else:
                z2_rows = keep.tile([P, PACK, n], BF16, name="z2_rows%d" % lo)
                nc.vector.tensor_tensor(z2_rows[:], at_n3[:], at_n4[:], ALU.max)
                nc.scalar.copy(by_runs, z2_rows[:].rearrange("p t (c i) -> p c t i", i=RUN))
            z2_mx = quantise(z2_woven[:], "z2_%d" % lo)
            z2_chunks.append(z2_mx)
            product(s_banks[0][:, lo:hi], z_first, 0, z2_mx)
            nc.scalar.activation(half_s_rows[0][:, lo:hi], s_banks[0][:, lo:hi], ACT.Copy, scale=half_s_scale)

        z_second = quantise(z_woven[:, PACK * P : 2 * PACK * P], "z_second", "at_n3")
        z_rest = quantise(z_woven[:, 2 * PACK * P :], "z_rest", "first_woven")
        for u, (z_mx, block) in ((1, (z_second, 0)), (2, (z_rest, 0)), (3, (z_rest, 1))):
            for (lo, hi), z2_mx in zip(QUERY_CHUNKS, z2_chunks):
                product(s_banks[u][:, lo:hi], z_mx, block, z2_mx)
            nc.scalar.activation(half_s_rows[u][:], s_banks[u][:], ACT.Copy, scale=half_s_scale)

        out_rows = out.rearrange("(p u) v -> p u v", u=PACK)
        for u in range(PACK):
            is_last = u == PACK - 1
            pieces = LAST_GATE_PIECES if is_last else GATE_HALVES
            at_n6 = keep.tile([P, V], F32, name="at_n6_%d" % u)
            half_diff = keep.tile([P, V], F32, name="half_diff%d" % u, tag="tanh%d" % (u - 1) if is_last else "half_diff%d" % u)
            tanh_rows = keep.tile([P, V], F32, name="tanh%d" % u)
            for lo, hi in GATE_HALVES:
                nc.vector.tensor_copy(at_n6[:, lo:hi], half_s_rows[u][:].indirect(entries(n6_t, lo, hi)))
            for lo, hi in pieces:
                nc.vector.tensor_tensor(
                    half_diff[:, lo:hi], half_s_rows[u][:].indirect(entries(n5_t, lo, hi)), at_n6[:, lo:hi], ALU.subtract
                )
                nc.scalar.activation(tanh_rows[:, lo:hi], half_diff[:, lo:hi], ACT.Tanh)
            for lo, hi in pieces if is_last else ((0, V),):
                gated = keep.tile([P, hi - lo], F32, name="gated%d_%d" % (u, lo))
                nc.vector.scalar_tensor_tensor(gated[:], tanh_rows[:, lo:hi], 1.0, half_s_rows[u][:, lo:hi], ALU.add, ALU.mult)
                nc.sync.dma_start(out_rows[:, u, lo:hi], gated[:])
